import numpy as np
import ml_dtypes


def mxq(x, axis, fmt="e4m3"):
    dtype, down = {"e4m3": (ml_dtypes.float8_e4m3fn, 7), "e5m2": (ml_dtypes.float8_e5m2, 14)}[fmt]
    v = np.moveaxis(np.asarray(x, np.float32).astype(ml_dtypes.bfloat16).astype(np.float64), axis, -1)
    blocks = v.reshape(v.shape[:-1] + (-1, 32))
    amax = np.abs(blocks).max(-1, keepdims=True)
    byte = np.maximum(np.where(amax > 0, np.frexp(amax)[1] - 1 + 127, 0) - down, 1)
    scale = np.exp2(byte - 127.0)
    codes = (blocks / scale).astype(np.float32).astype(dtype).astype(np.float64)
    return np.moveaxis((codes * scale).reshape(v.shape), -1, axis)


WIDE = False


def mx_kscale(k):
    if not WIDE:
        return np.ones(k)
    levels = np.array([10, -10, 5, -5, 0])
    if k % 512:
        return np.exp2(np.random.permutation(np.resize(levels, k // 32))).repeat(32)
    a = np.empty((k // 512, 16))
    for p in range(k // 512):
        a[p, :8] = np.random.permutation(np.resize(levels, 8))
        for g in range(8):
            far = levels[np.abs(levels - a[p, g]) >= 10]
            a[p, g + 8] = far[np.random.randint(len(far))]
    return np.exp2(a.ravel()).repeat(32)


def f64(x):
    return np.asarray(x).astype(np.float64)


def striped(idx):
    return np.tile(idx.reshape(-1, 16).T, (8, 1)).astype(np.uint16)


def unstriped(offs):
    return offs[:16].T.reshape(-1).astype(np.int64)


def pack_weight(w):
    k, n = w.shape
    w = f64(np.asarray(w, np.float32).astype(ml_dtypes.bfloat16)).reshape(k // 32, 32, n)
    amax = np.abs(w).max(1)
    byte = np.clip(np.where(amax > 0, np.frexp(amax)[1] - 1 + 127 - 7, 1), 1, 254)
    scaled = (w * np.exp2(127.0 - byte)[:, None, :]).reshape(k, n).astype(np.float32)
    words = np.ascontiguousarray(scaled.reshape(k // 512, 128, 4, n).transpose(0, 1, 3, 2)).astype(ml_dtypes.float8_e4m3fn).view(np.uint8)
    return words, np.ascontiguousarray(byte.astype(np.uint8).reshape(k // 512, 16, n))


def unpack_weight(words, scales):
    g, p, n, _ = words.shape
    vals = np.ascontiguousarray(words).view(ml_dtypes.float8_e4m3fn).astype(np.float64) * np.repeat(np.exp2(scales.astype(np.float64) - 127.0), 8, axis=1)[..., None]
    return vals.transpose(0, 1, 3, 2).reshape(g * 512, n)


K, T, E, C, N = 2048, 512, 8, 128, 384
TOP = 3
PAD = 64


def by_expert(wq, xq):
    return np.concatenate([wq[e].T @ xq[:, e * C:(e + 1) * C] for e in range(E)], axis=1)


def setup_inputs():
    n = np.random.standard_normal
    s = mx_kscale(K)[:, None]
    slot_token = np.empty(E * C, np.int64); pos = np.tile(E * C + np.arange(T) % PAD, (TOP, 1)); taken = np.zeros(T, np.int64)
    liked = np.random.randn(T)
    for e in np.random.permutation(E):
        free = np.flatnonzero(taken < TOP); pick = np.random.permutation(free[np.argsort(-(liked[free] + np.random.gumbel(size=free.size)))[:C]]); slot_token[e * C:(e + 1) * C] = pick
        pos[taken[pick], pick] = e * C + np.arange(C); taken[pick] += 1
    g = np.random.uniform(0.2, 0.8, (TOP, T))
    packed = [pack_weight(m) for m in n((E, K, N)) / np.sqrt(K) / s[None]]
    return {
        "xT": (n((K, T)) * s).astype(np.float32),
        "w_words": np.stack([m[0] for m in packed]),
        "w_scales": np.stack([m[1] for m in packed]),
        "gate": np.stack([np.tile(r, (N, 1)) for r in g]).astype(np.float32),
        "offs": striped(slot_token),
        "pos1": striped(pos[0]),
        "pos2": striped(pos[1]),
        "pos3": striped(pos[2]),
    }


def reference(xT, w_words, w_scales, gate, offs, pos1, pos2, pos3):
    idx = unstriped(offs)
    w = np.stack([unpack_weight(w_words[e], w_scales[e]) for e in range(E)])
    xq = mxq(f64(xT)[:, idx], 0, "e4m3")
    y = by_expert(w, xq)
    y = np.concatenate([y, np.zeros((N, PAD))], axis=1)
    return sum(f64(gate[r]) * y[:, unstriped(p)] for r, p in enumerate((pos1, pos2, pos3)))

@@ -1,0 +1,168 @@
+from contextlib import ExitStack
+
+import concourse.mybir as mybir
+
+K, T, E, C, N = 2048, 512, 8, 128, 384
+TOP = 3
+PAD = 64
+SLOTS = E * C
+FLOPS = 2 * K * N * SLOTS
+
+F32 = mybir.dt.float32
+BF16 = mybir.dt.bfloat16
+I32 = mybir.dt.int32
+U32 = mybir.dt.uint32
+U16 = mybir.dt.uint16
+U8 = mybir.dt.uint8
+FP8X4 = mybir.dt.float8_e4m3fn_x4
+COPY = mybir.ActivationFunctionType.Copy
+MULT = mybir.AluOpType.mult
+ADD = mybir.AluOpType.add
+
+P = 128
+PACK = 4
+PASSES = K // (P * PACK)
+HALF = T // 2
+BLOCKS = N // P
+WIDE = 1408
+NARROW = 704
+GROUPS = ((0, 4), (4, 7), (7, 8))
+V_SHARE = 160
+
+
+def interleave(dst, src):
+    return dst.rearrange("p (c i) j -> p c j i", i=4), src.rearrange("p j (c i) -> p c j i", i=4)
+
+
+def tile_moe_ecr_lin_none_kernel(tc, xT, w_words, w_scales, gate, offs, pos1, pos2, pos3, out):
+    nc = tc.nc
+    with ExitStack() as ctx:
+        lists = ctx.enter_context(tc.tile_pool(name="lists", bufs=1))
+        keep = ctx.enter_context(tc.tile_pool(name="keep", bufs=1))
+        work = ctx.enter_context(tc.tile_pool(name="work", bufs=2))
+        psum = ctx.enter_context(tc.psum_pool(name="psum", bufs=8))
+
+        offs_sb = lists.tile([P, SLOTS // 16], U16, name="offs_sb")
+        pos_sb = [lists.tile([P, T // 16], U16, name="pos_sb%d" % r) for r in range(TOP)]
+
+        w_scale_sb = keep.tile([P, E * N], U8, name="w_scale_sb", align_bytes=64)
+        tok_words = keep.tile([P, (PASSES - 1) * T + WIDE], U32, name="tok_words", align_bytes=64)
+        tok_scales = keep.tile([P, NARROW], U8, name="tok_scales", align_bytes=64)
+        slot_words = [keep.tile([P, SLOTS], U32, name="slot_words%d" % a, align_bytes=64) for a in range(PASSES)]
+        slot_scales = keep.tile([P, SLOTS], U8, name="slot_scales", align_bytes=64)
+        y = [keep.tile([P, SLOTS + PAD], F32, name="y%d" % b) for b in range(BLOCKS)]
+        gate_sb = keep.tile([P, TOP, T], F32, name="gate_sb")
+        x_raw = [[keep.tile([P, PACK, HALF], F32, name="x_raw%d_%d" % (a, h)) for h in range(2)] for a in range(PASSES)]
+        x_bf = [keep.tile([P, T, PACK], BF16, name="x_bf%d" % a, align_bytes=64) for a in range(PASSES)]
+        w_sb = [[keep.tile([P, (e1 - e0) * PASSES * P * PACK], U8, name="w_sb%d_%d" % (b, e0), align_bytes=64)
+                 for e0, e1 in GROUPS] for b in range(BLOCKS)]
+
+        nc.vector.memset(w_scale_sb[:].bitcast(I32), 0)
+        nc.vector.memset(tok_scales[:].bitcast(I32), 0)
+        nc.vector.memset(tok_words[:, PASSES * T:].bitcast(I32), 0)
+        nc.vector.memset(y[0][:, SLOTS:], 0.0)
+        for b in range(1, BLOCKS):
+            nc.scalar.activation(y[b][:, SLOTS:], y[0][:, SLOTS:], COPY)
+
+        def load_x(a, h):
+            rows = xT[a * P * PACK:(a + 1) * P * PACK, h * HALF:(h + 1) * HALF]
+            nc.sync.dma_start(out=x_raw[a][h][:], in_=rows.rearrange("(p j) t -> p j t", j=PACK))
+
+        def load_w_scales(q):
+            quad, j = divmod(q, 4)
+            dst = w_scale_sb[:].bitcast(I32)[32 * quad + j:32 * quad + 16:4, :]
+            src = w_scales.rearrange("e a q n -> q a e n")[q].bitcast(I32)
+            nc.sync.dma_start(out=dst.rearrange("a (e n) -> a e n", e=E), in_=src)
+
+        def load_w(b, g):
+            e0, e1 = GROUPS[g]
+            src = w_words.rearrange("e a p n r -> p (e a) (n r)")
+            src = src[:, e0 * PASSES:e1 * PASSES, b * P * PACK:(b + 1) * P * PACK].bitcast(I32)
+            nc.sync.dma_start(out=w_sb[b][g][:].bitcast(I32).rearrange("p (m c) -> p m c", c=P), in_=src)
+
+        load_x(0, 0)
+        load_x(0, 1)
+        nc.sync.dma_start(offs_sb[:], offs)
+        big = [(load_x, a, h) for a in range(1, PASSES) for h in range(2)] + [(load_w, 0, 0), (load_w, 0, 1)]
+        for i, (load, u, v) in enumerate(big):
+            load(u, v)
+            load_w_scales(2 * i)
+            load_w_scales(2 * i + 1)
+        load_w(0, 2)
+        for r, pos in enumerate((pos1, pos2, pos3)):
+            nc.sync.dma_start(pos_sb[r][:], pos)
+        nc.sync.dma_start(out=gate_sb[:], in_=gate[:, 0:P, :].rearrange("r p t -> p r t"))
+        for b in range(1, BLOCKS):
+            for g in range(len(GROUPS)):
+                load_w(b, g)
+
+        def word_col(a):
+            return (PASSES - 1 - a) * T
+
+        def quantize(a, t0, t1):
+            nc.vector.quantize_mx(
+                out=tok_words[:, word_col(a) + t0:word_col(a) + t1].bitcast(FP8X4),
+                scales=tok_scales[4 * a:, t0:t1],
+                in_=x_bf[a][:, t0:t1, :].rearrange("p t j -> p (t j)"),
+            )
+
+        def gather_words(a, s0, s1, window):
+            src = tok_words[:, word_col(a):word_col(a) + window]
+            nc.vector.tensor_copy(slot_words[a][:, s0:s1], src.indirect(offs_sb[:, s0 // 16:s1 // 16]))
+
+        dst, src = interleave(x_bf[0][:, 0:HALF, :], x_raw[0][0][:])
+        nc.vector.tensor_copy(out=dst, in_=src)
+        quantize(0, 0, HALF)
+        dst, src = interleave(x_bf[0][:, HALF:HALF + V_SHARE, :], x_raw[0][1][:, :, 0:V_SHARE])
+        nc.vector.tensor_copy(out=dst, in_=src)
+        dst, src = interleave(x_bf[0][:, HALF + V_SHARE:, :], x_raw[0][1][:, :, V_SHARE:])
+        nc.scalar.activation(dst, src, COPY)
+        quantize(0, HALF, T)
+        for a in range(1, PASSES):
+            gather_words(a - 1, 0, SLOTS, WIDE)
+            for h in range(2):
+                dst, src = interleave(x_bf[a][:, h * HALF:(h + 1) * HALF, :], x_raw[a][h][:])
+                nc.scalar.activation(dst, src, COPY)
+            quantize(a, 0, T)
+        last = PASSES - 1
+        for h in range(2):
+            s0, s1 = h * T, (h + 1) * T
+            nc.vector.tensor_copy(slot_scales[:, s0:s1], tok_scales[:].indirect(offs_sb[:, s0 // 16:s1 // 16]))
+            if h == 0:
+                gather_words(last, s0, s1, NARROW)
+            else:
+                gather_words(last, s0, s1 - C, T)
+                gather_words(last, s1 - C, s1, T)
+
+        def experts(b):
+            for g, (e0, e1) in enumerate(GROUPS):
+                acc = psum.tile([P, (e1 - e0) * C], F32, name="acc")
+                for e in range(e0, e1):
+                    for a in range(PASSES):
+                        m = (e - e0) * PASSES + a
+                        nc.tensor.matmul_mx(
+                            out=acc[:, (e - e0) * C:(e - e0 + 1) * C],
+                            lhsT=w_sb[b][g][:, m * P * PACK:(m + 1) * P * PACK].bitcast(FP8X4),
+                            lhsT_scale=w_scale_sb[4 * a:, e * N + b * P:e * N + (b + 1) * P],
+                            rhs=slot_words[a][:, e * C:(e + 1) * C].bitcast(FP8X4),
+                            rhs_scale=slot_scales[4 * a:, e * C:(e + 1) * C],
+                            start=(a == 0),
+                            stop=(a == PASSES - 1),
+                        )
+                nc.scalar.activation(y[b][:, e0 * C:e1 * C], acc[:], COPY)
+
+        def combine(b):
+            terms = []
+            for r in range(TOP):
+                term = work.tile([P, T], F32, name="term%d" % r)
+                nc.vector.tensor_tensor(term[:], y[b][:].indirect(pos_sb[r][:]), gate_sb[:, r, :], MULT)
+                terms.append(term)
+            part = work.tile([P, T], F32, name="part")
+            nc.vector.tensor_tensor(part[:], terms[0][:], terms[1][:], ADD)
+            total = work.tile([P, T], F32, name="total")
+            nc.vector.tensor_tensor(total[:], part[:], terms[2][:], ADD)
+            nc.sync.dma_start(out=out[b * P:(b + 1) * P, :], in_=total[:])
+
+        for b in range(BLOCKS):
+            experts(b)
+            combine(b)

@@ -1,6 +1,7 @@
 from contextlib import ExitStack
 
 import concourse.mybir as mybir
+from concourse.masks import make_identity
 
 K, T, E, C, N = 2048, 512, 8, 128, 384
 TOP = 3
@@ -25,13 +26,11 @@ PASSES = K // (P * PACK)
 HALF = T // 2
 BLOCKS = N // P
 WIDE = 1408
-NARROW = 704
-GROUPS = ((0, 4), (4, 7), (7, 8))
-V_SHARE = 160
-
-
-def interleave(dst, src):
-    return dst.rearrange("p (c i) j -> p c j i", i=4), src.rearrange("p j (c i) -> p c j i", i=4)
+V_SHARE0 = 160
+V_SHARE1 = 192
+PIECES = ((0, 4, 0, 1), (4, 6, 0, 1), (6, 7, 0, 2), (7, 8, 0, 2),
+          (0, 2, 1, 3), (2, 4, 1, 2), (4, 5, 1, 2), (5, 6, 1, 2),
+          (2, 4, 2, 3), (4, 6, 2, 3), (6, 7, 2, 3), (7, 8, 2, 3))
 
 
 def tile_moe_ecr_lin_none_kernel(tc, xT, w_words, w_scales, gate, offs, pos1, pos2, pos3, out):
@@ -39,24 +38,27 @@ def tile_moe_ecr_lin_none_kernel(tc, xT, w_words, w_scales, gate, offs, pos1, po
     with ExitStack() as ctx:
         lists = ctx.enter_context(tc.tile_pool(name="lists", bufs=1))
         keep = ctx.enter_context(tc.tile_pool(name="keep", bufs=1))
-        work = ctx.enter_context(tc.tile_pool(name="work", bufs=2))
-        psum = ctx.enter_context(tc.psum_pool(name="psum", bufs=8))
+        psum = ctx.enter_context(tc.psum_pool(name="psum", bufs=1))
 
         offs_sb = lists.tile([P, SLOTS // 16], U16, name="offs_sb")
         pos_sb = [lists.tile([P, T // 16], U16, name="pos_sb%d" % r) for r in range(TOP)]
 
         w_scale_sb = keep.tile([P, E * N], U8, name="w_scale_sb", align_bytes=64)
         tok_words = keep.tile([P, (PASSES - 1) * T + WIDE], U32, name="tok_words", align_bytes=64)
-        tok_scales = keep.tile([P, NARROW], U8, name="tok_scales", align_bytes=64)
+        tok_scales = keep.tile([P, T], U8, name="tok_scales", align_bytes=64)
         slot_words = [keep.tile([P, SLOTS], U32, name="slot_words%d" % a, align_bytes=64) for a in range(PASSES)]
         slot_scales = keep.tile([P, SLOTS], U8, name="slot_scales", align_bytes=64)
         y = [keep.tile([P, SLOTS + PAD], F32, name="y%d" % b) for b in range(BLOCKS)]
-        gate_sb = keep.tile([P, TOP, T], F32, name="gate_sb")
-        x_raw = [[keep.tile([P, PACK, HALF], F32, name="x_raw%d_%d" % (a, h)) for h in range(2)] for a in range(PASSES)]
+        gate_cols = keep.tile([P, TOP, T // P], F32, name="gate_cols")
+        gate_sb = [keep.tile([P, T], F32, name="gate_sb%d" % r) for r in range(TOP)]
+        ident = keep.tile([P, P], F32, name="ident")
+        x_parts = [(0, 0, HALF), (0, HALF, T)] + [(a, 0, T) for a in range(1, PASSES)]
+        x_raw = [keep.tile([P, PACK, t1 - t0], F32, name="x_raw%d_%d" % (a, t0)) for a, t0, t1 in x_parts]
         x_bf = [keep.tile([P, T, PACK], BF16, name="x_bf%d" % a, align_bytes=64) for a in range(PASSES)]
-        w_sb = [[keep.tile([P, (e1 - e0) * PASSES * P * PACK], U8, name="w_sb%d_%d" % (b, e0), align_bytes=64)
-                 for e0, e1 in GROUPS] for b in range(BLOCKS)]
+        w_sb = [keep.tile([P, (e1 - e0) * PASSES * (b1 - b0) * P * PACK], U8, name="w_sb%d" % i, align_bytes=64)
+                for i, (e0, e1, b0, b1) in enumerate(PIECES)]
 
+        make_identity(nc, ident[:])
         nc.vector.memset(w_scale_sb[:].bitcast(I32), 0)
         nc.vector.memset(tok_scales[:].bitcast(I32), 0)
         nc.vector.memset(tok_words[:, PASSES * T:].bitcast(I32), 0)
@@ -64,40 +66,50 @@ def tile_moe_ecr_lin_none_kernel(tc, xT, w_words, w_scales, gate, offs, pos1, po
         for b in range(1, BLOCKS):
             nc.scalar.activation(y[b][:, SLOTS:], y[0][:, SLOTS:], COPY)
 
-        def load_x(a, h):
-            rows = xT[a * P * PACK:(a + 1) * P * PACK, h * HALF:(h + 1) * HALF]
-            nc.sync.dma_start(out=x_raw[a][h][:], in_=rows.rearrange("(p j) t -> p j t", j=PACK))
+        def load_x(i):
+            a, t0, t1 = x_parts[i]
+            rows = xT[a * P * PACK:(a + 1) * P * PACK, t0:t1]
+            nc.sync.dma_start(out=x_raw[i][:], in_=rows.rearrange("(p j) t -> p j t", j=PACK))
 
-        def load_w_scales(q):
-            quad, j = divmod(q, 4)
-            dst = w_scale_sb[:].bitcast(I32)[32 * quad + j:32 * quad + 16:4, :]
-            src = w_scales.rearrange("e a q n -> q a e n")[q].bitcast(I32)
-            nc.sync.dma_start(out=dst.rearrange("a (e n) -> a e n", e=E), in_=src)
+        def load_w_scales(quad):
+            for j in range(4):
+                dst = w_scale_sb[:].bitcast(I32)[32 * quad + j:32 * quad + 16:4, :]
+                src = w_scales.rearrange("e a q n -> q a e n")[4 * quad + j].bitcast(I32)
+                nc.sync.dma_start(out=dst.rearrange("a (e n) -> a e n", e=E), in_=src)
 
-        def load_w(b, g):
-            e0, e1 = GROUPS[g]
+        def load_w(i):
+            e0, e1, b0, b1 = PIECES[i]
             src = w_words.rearrange("e a p n r -> p (e a) (n r)")
-            src = src[:, e0 * PASSES:e1 * PASSES, b * P * PACK:(b + 1) * P * PACK].bitcast(I32)
-            nc.sync.dma_start(out=w_sb[b][g][:].bitcast(I32).rearrange("p (m c) -> p m c", c=P), in_=src)
+            src = src[:, e0 * PASSES:e1 * PASSES, b0 * P * PACK:b1 * P * PACK].bitcast(I32)
+            nc.sync.dma_start(out=w_sb[i][:].bitcast(I32).rearrange("p (m c) -> p m c", c=(b1 - b0) * P), in_=src)
 
-        load_x(0, 0)
-        load_x(0, 1)
+        load_x(0)
+        load_x(1)
         nc.sync.dma_start(offs_sb[:], offs)
-        big = [(load_x, a, h) for a in range(1, PASSES) for h in range(2)] + [(load_w, 0, 0), (load_w, 0, 1)]
-        for i, (load, u, v) in enumerate(big):
-            load(u, v)
-            load_w_scales(2 * i)
-            load_w_scales(2 * i + 1)
-        load_w(0, 2)
+        nc.sync.dma_start(out=gate_cols[:], in_=gate[:, 0, :].rearrange("r (p c) -> p r c", p=P))
+        for quad in range(3):
+            load_x(2 + quad)
+            load_w_scales(quad)
+        load_w(0)
+        load_w_scales(3)
         for r, pos in enumerate((pos1, pos2, pos3)):
             nc.sync.dma_start(pos_sb[r][:], pos)
-        nc.sync.dma_start(out=gate_sb[:], in_=gate[:, 0:P, :].rearrange("r p t -> p r t"))
-        for b in range(1, BLOCKS):
-            for g in range(len(GROUPS)):
-                load_w(b, g)
+        for i in range(1, len(PIECES)):
+            load_w(i)
 
         def word_col(a):
             return (PASSES - 1 - a) * T
+
+        def gather_words(a, s0, s1, window):
+            src = tok_words[:, word_col(a):word_col(a) + window]
+            nc.vector.tensor_copy(slot_words[a][:, s0:s1], src.indirect(offs_sb[:, s0 // 16:s1 // 16]))
+
+        def scalar_copy(dst, src):
+            nc.scalar.activation(dst, src, COPY)
+
+        def cast(copy, i, c0, c1):
+            a, t0, t1 = x_parts[i]
+            copy(x_bf[a][:, t0 + c0:t0 + c1, :], x_raw[i][:, :, c0:c1].rearrange("p j t -> p t j"))
 
         def quantize(a, t0, t1):
             nc.vector.quantize_mx(
@@ -106,63 +118,101 @@ def tile_moe_ecr_lin_none_kernel(tc, xT, w_words, w_scales, gate, offs, pos1, po
                 in_=x_bf[a][:, t0:t1, :].rearrange("p t j -> p (t j)"),
             )
 
-        def gather_words(a, s0, s1, window):
-            src = tok_words[:, word_col(a):word_col(a) + window]
-            nc.vector.tensor_copy(slot_words[a][:, s0:s1], src.indirect(offs_sb[:, s0 // 16:s1 // 16]))
-
-        dst, src = interleave(x_bf[0][:, 0:HALF, :], x_raw[0][0][:])
-        nc.vector.tensor_copy(out=dst, in_=src)
+        cast(nc.vector.tensor_copy, 0, 0, HALF)
         quantize(0, 0, HALF)
-        dst, src = interleave(x_bf[0][:, HALF:HALF + V_SHARE, :], x_raw[0][1][:, :, 0:V_SHARE])
-        nc.vector.tensor_copy(out=dst, in_=src)
-        dst, src = interleave(x_bf[0][:, HALF + V_SHARE:, :], x_raw[0][1][:, :, V_SHARE:])
-        nc.scalar.activation(dst, src, COPY)
+        cast(nc.vector.tensor_copy, 1, 0, V_SHARE0)
+        cast(scalar_copy, 1, V_SHARE0, HALF)
         quantize(0, HALF, T)
-        for a in range(1, PASSES):
+        gather_words(0, 0, SLOTS, WIDE)
+        cast(scalar_copy, 2, V_SHARE1, T)
+        cast(nc.vector.tensor_copy, 2, 0, V_SHARE1)
+        quantize(1, 0, T)
+        for a in range(2, PASSES):
             gather_words(a - 1, 0, SLOTS, WIDE)
-            for h in range(2):
-                dst, src = interleave(x_bf[a][:, h * HALF:(h + 1) * HALF, :], x_raw[a][h][:])
-                nc.scalar.activation(dst, src, COPY)
+            cast(scalar_copy, a + 1, 0, T)
             quantize(a, 0, T)
         last = PASSES - 1
-        for h in range(2):
-            s0, s1 = h * T, (h + 1) * T
+        for s0 in range(0, SLOTS, 2 * C):
+            s1 = s0 + 2 * C
             nc.vector.tensor_copy(slot_scales[:, s0:s1], tok_scales[:].indirect(offs_sb[:, s0 // 16:s1 // 16]))
-            if h == 0:
-                gather_words(last, s0, s1, NARROW)
+            if s1 < SLOTS:
+                gather_words(last, s0, s1, T)
             else:
-                gather_words(last, s0, s1 - C, T)
-                gather_words(last, s1 - C, s1, T)
+                gather_words(last, s0, s0 + C, T)
+                gather_words(last, s0 + C, s1, T)
 
-        def experts(b):
-            for g, (e0, e1) in enumerate(GROUPS):
-                acc = psum.tile([P, (e1 - e0) * C], F32, name="acc")
+        for r in range(TOP):
+            spread = psum.tile([P, T // P, P], F32, name="spread", tag="back", bufs=2)
+            for c in range(T // P):
+                nc.tensor.transpose(spread[:, c, :], gate_cols[:, r, c:c + 1].to_broadcast([P, P]), ident[:])
+            nc.scalar.activation(gate_sb[r][:].rearrange("m (p c) -> m p c", p=P), spread[:].rearrange("m c p -> m p c"), COPY)
+
+        def experts(b, pieces, tag, bufs, copy):
+            first, end = PIECES[pieces[0]][0], PIECES[pieces[-1]][1]
+            acc = psum.tile([P, (end - first) * C], F32, name="acc", tag=tag, bufs=bufs)
+            for i in pieces:
+                e0, e1, b0, b1 = PIECES[i]
                 for e in range(e0, e1):
                     for a in range(PASSES):
-                        m = (e - e0) * PASSES + a
+                        col = (((e - e0) * PASSES + a) * (b1 - b0) + b - b0) * P * PACK
                         nc.tensor.matmul_mx(
-                            out=acc[:, (e - e0) * C:(e - e0 + 1) * C],
-                            lhsT=w_sb[b][g][:, m * P * PACK:(m + 1) * P * PACK].bitcast(FP8X4),
+                            out=acc[:, (e - first) * C:(e - first + 1) * C],
+                            lhsT=w_sb[i][:, col:col + P * PACK].bitcast(FP8X4),
                             lhsT_scale=w_scale_sb[4 * a:, e * N + b * P:e * N + (b + 1) * P],
                             rhs=slot_words[a][:, e * C:(e + 1) * C].bitcast(FP8X4),
                             rhs_scale=slot_scales[4 * a:, e * C:(e + 1) * C],
                             start=(a == 0),
                             stop=(a == PASSES - 1),
                         )
-                nc.scalar.activation(y[b][:, e0 * C:e1 * C], acc[:], COPY)
+            copy(y[b][:, first * C:end * C], acc[:])
 
-        def combine(b):
-            terms = []
-            for r in range(TOP):
-                term = work.tile([P, T], F32, name="term%d" % r)
-                nc.vector.tensor_tensor(term[:], y[b][:].indirect(pos_sb[r][:]), gate_sb[:, r, :], MULT)
-                terms.append(term)
-            part = work.tile([P, T], F32, name="part")
-            nc.vector.tensor_tensor(part[:], terms[0][:], terms[1][:], ADD)
-            total = work.tile([P, T], F32, name="total")
-            nc.vector.tensor_tensor(total[:], part[:], terms[2][:], ADD)
-            nc.sync.dma_start(out=out[b * P:(b + 1) * P, :], in_=total[:])
+        def gated(b, r, term, t0, t1):
+            nc.vector.tensor_tensor(term[:, t0:t1], y[b][:].indirect(pos_sb[r][:, t0 // 16:t1 // 16]), gate_sb[r][:, t0:t1], MULT)
 
-        for b in range(BLOCKS):
-            experts(b)
-            combine(b)
+        for i in range(3):
+            experts(0, [i], "acc", 3, scalar_copy)
+        experts(0, [3], "after0", 1, nc.vector.tensor_copy)
+        experts(1, [2, 3], "after0", 1, scalar_copy)
+        experts(1, [4, 5], "acc", 3, scalar_copy)
+        experts(1, [6], "acc", 3, scalar_copy)
+        experts(1, [7], "late0", 1, scalar_copy)
+        experts(2, [4], "late0", 1, scalar_copy)
+        for i in range(8, 10):
+            experts(2, [i], "acc", 3, scalar_copy)
+        experts(2, [10], "after0", 1, scalar_copy)
+        experts(2, [11], "late1", 1, scalar_copy)
+
+        terms = [[keep.tile([P, T], F32, name="term%d_%d" % (b, r)) for r in range(TOP)] for b in range(BLOCKS)]
+        for b in range(BLOCKS - 1):
+            gated(b, 0, terms[b][0], 0, T)
+            gated(b, 1, terms[b][1], 0, T)
+            gated(b, 2, terms[b][2], 0, HALF)
+            gated(b, 2, terms[b][2], HALF, T)
+
+        for b in range(BLOCKS - 1):
+            turned = psum.tile([P, T // P, P], F32, name="turned", tag="late%d" % b, bufs=1)
+            for c in range(T // P):
+                for r in range(TOP):
+                    nc.tensor.matmul(turned[:, c, :], lhsT=terms[b][r][:, c * P:(c + 1) * P], rhs=ident[:],
+                                     is_transpose=True, start=(r == 0), stop=(r == TOP - 1))
+            turned_sb = keep.tile([P, T // P, P], F32, name="turned_sb%d" % b)
+            nc.scalar.activation(turned_sb[:], turned[:], COPY)
+            back = psum.tile([P, T], F32, name="back", tag=("after0", "back")[b], bufs=(1, 2)[b])
+            for c in range(T // P):
+                nc.tensor.transpose(back[:, c * P:(c + 1) * P], turned_sb[:, c, :], ident[:])
+            total = keep.tile([P, T], F32, name="total%d" % b)
+            nc.scalar.activation(total[:], back[:], COPY)
+            nc.scalar.dma_start(out=out[b * P:(b + 1) * P, :], in_=total[:])
+
+        b = BLOCKS - 1
+        part = keep.tile([P, T], F32, name="part")
+        total = keep.tile([P, T], F32, name="total_last")
+        gated(b, 0, terms[b][0], 0, T)
+        gated(b, 1, terms[b][1], 0, T)
+        gated(b, 2, terms[b][2], 0, HALF)
+        nc.vector.tensor_tensor(part[:], terms[b][0][:], terms[b][1][:], ADD)
+        gated(b, 2, terms[b][2], HALF, T)
+        for h in range(2):
+            cols = slice(h * HALF, (h + 1) * HALF)
+            nc.vector.tensor_tensor(total[:, cols], part[:, cols], terms[b][2][:, cols], ADD)
+            nc.sync.dma_start(out=out[b * P:(b + 1) * P, cols], in_=total[:, cols])

from contextlib import ExitStack

import concourse.mybir as mybir
from concourse.masks import make_identity

K, T, E, C, N = 2048, 512, 8, 128, 384
TOP = 3
PAD = 64
SLOTS = E * C
FLOPS = 2 * K * N * SLOTS

F32 = mybir.dt.float32
BF16 = mybir.dt.bfloat16
I32 = mybir.dt.int32
U32 = mybir.dt.uint32
U16 = mybir.dt.uint16
U8 = mybir.dt.uint8
FP8X4 = mybir.dt.float8_e4m3fn_x4
COPY = mybir.ActivationFunctionType.Copy
MULT = mybir.AluOpType.mult
ADD = mybir.AluOpType.add

P = 128
PACK = 4
PASSES = K // (P * PACK)
HALF = T // 2
BLOCKS = N // P
WIDE = 1408
V_SHARE0 = 160
V_SHARE1 = 192
PIECES = ((0, 4, 0, 1), (4, 6, 0, 1), (6, 7, 0, 2), (7, 8, 0, 2),
          (0, 2, 1, 3), (2, 4, 1, 2), (4, 5, 1, 2), (5, 6, 1, 2),
          (2, 4, 2, 3), (4, 6, 2, 3), (6, 7, 2, 3), (7, 8, 2, 3))


def tile_moe_ecr_lin_none_kernel(tc, xT, w_words, w_scales, gate, offs, pos1, pos2, pos3, out):
    nc = tc.nc
    with ExitStack() as ctx:
        lists = ctx.enter_context(tc.tile_pool(name="lists", bufs=1))
        keep = ctx.enter_context(tc.tile_pool(name="keep", bufs=1))
        psum = ctx.enter_context(tc.psum_pool(name="psum", bufs=1))

        offs_sb = lists.tile([P, SLOTS // 16], U16, name="offs_sb")
        pos_sb = [lists.tile([P, T // 16], U16, name="pos_sb%d" % r) for r in range(TOP)]

        w_scale_sb = keep.tile([P, E * N], U8, name="w_scale_sb", align_bytes=64)
        tok_words = keep.tile([P, (PASSES - 1) * T + WIDE], U32, name="tok_words", align_bytes=64)
        tok_scales = keep.tile([P, T], U8, name="tok_scales", align_bytes=64)
        slot_words = [keep.tile([P, SLOTS], U32, name="slot_words%d" % a, align_bytes=64) for a in range(PASSES)]
        slot_scales = keep.tile([P, SLOTS], U8, name="slot_scales", align_bytes=64)
        y = [keep.tile([P, SLOTS + PAD], F32, name="y%d" % b) for b in range(BLOCKS)]
        gate_cols = keep.tile([P, TOP, T // P], F32, name="gate_cols")
        gate_sb = [keep.tile([P, T], F32, name="gate_sb%d" % r) for r in range(TOP)]
        ident = keep.tile([P, P], F32, name="ident")
        x_parts = [(0, 0, HALF), (0, HALF, T)] + [(a, 0, T) for a in range(1, PASSES)]
        x_raw = [keep.tile([P, PACK, t1 - t0], F32, name="x_raw%d_%d" % (a, t0)) for a, t0, t1 in x_parts]
        x_bf = [keep.tile([P, T, PACK], BF16, name="x_bf%d" % a, align_bytes=64) for a in range(PASSES)]
        w_sb = [keep.tile([P, (e1 - e0) * PASSES * (b1 - b0) * P * PACK], U8, name="w_sb%d" % i, align_bytes=64)
                for i, (e0, e1, b0, b1) in enumerate(PIECES)]

        make_identity(nc, ident[:])
        nc.vector.memset(w_scale_sb[:].bitcast(I32), 0)
        nc.vector.memset(tok_scales[:].bitcast(I32), 0)
        nc.vector.memset(tok_words[:, PASSES * T:].bitcast(I32), 0)
        nc.vector.memset(y[0][:, SLOTS:], 0.0)
        for b in range(1, BLOCKS):
            nc.scalar.activation(y[b][:, SLOTS:], y[0][:, SLOTS:], COPY)

        def load_x(i):
            a, t0, t1 = x_parts[i]
            rows = xT[a * P * PACK:(a + 1) * P * PACK, t0:t1]
            nc.sync.dma_start(out=x_raw[i][:], in_=rows.rearrange("(p j) t -> p j t", j=PACK))

        def load_w_scales(quad):
            for j in range(4):
                dst = w_scale_sb[:].bitcast(I32)[32 * quad + j:32 * quad + 16:4, :]
                src = w_scales.rearrange("e a q n -> q a e n")[4 * quad + j].bitcast(I32)
                nc.sync.dma_start(out=dst.rearrange("a (e n) -> a e n", e=E), in_=src)

        def load_w(i):
            e0, e1, b0, b1 = PIECES[i]
            src = w_words.rearrange("e a p n r -> p (e a) (n r)")
            src = src[:, e0 * PASSES:e1 * PASSES, b0 * P * PACK:b1 * P * PACK].bitcast(I32)
            nc.sync.dma_start(out=w_sb[i][:].bitcast(I32).rearrange("p (m c) -> p m c", c=(b1 - b0) * P), in_=src)

        load_x(0)
        load_x(1)
        nc.sync.dma_start(offs_sb[:], offs)
        nc.sync.dma_start(out=gate_cols[:], in_=gate[:, 0, :].rearrange("r (p c) -> p r c", p=P))
        for quad in range(3):
            load_x(2 + quad)
            load_w_scales(quad)
        load_w(0)
        load_w_scales(3)
        for r, pos in enumerate((pos1, pos2, pos3)):
            nc.sync.dma_start(pos_sb[r][:], pos)
        for i in range(1, len(PIECES)):
            load_w(i)

        def word_col(a):
            return (PASSES - 1 - a) * T

        def gather_words(a, s0, s1, window):
            src = tok_words[:, word_col(a):word_col(a) + window]
            nc.vector.tensor_copy(slot_words[a][:, s0:s1], src.indirect(offs_sb[:, s0 // 16:s1 // 16]))

        def scalar_copy(dst, src):
            nc.scalar.activation(dst, src, COPY)

        def cast(copy, i, c0, c1):
            a, t0, t1 = x_parts[i]
            copy(x_bf[a][:, t0 + c0:t0 + c1, :], x_raw[i][:, :, c0:c1].rearrange("p j t -> p t j"))

        def quantize(a, t0, t1):
            nc.vector.quantize_mx(
                out=tok_words[:, word_col(a) + t0:word_col(a) + t1].bitcast(FP8X4),
                scales=tok_scales[4 * a:, t0:t1],
                in_=x_bf[a][:, t0:t1, :].rearrange("p t j -> p (t j)"),
            )

        cast(nc.vector.tensor_copy, 0, 0, HALF)
        quantize(0, 0, HALF)
        cast(nc.vector.tensor_copy, 1, 0, V_SHARE0)
        cast(scalar_copy, 1, V_SHARE0, HALF)
        quantize(0, HALF, T)
        gather_words(0, 0, SLOTS, WIDE)
        cast(scalar_copy, 2, V_SHARE1, T)
        cast(nc.vector.tensor_copy, 2, 0, V_SHARE1)
        quantize(1, 0, T)
        for a in range(2, PASSES):
            gather_words(a - 1, 0, SLOTS, WIDE)
            cast(scalar_copy, a + 1, 0, T)
            quantize(a, 0, T)
        last = PASSES - 1
        for s0 in range(0, SLOTS, 2 * C):
            s1 = s0 + 2 * C
            nc.vector.tensor_copy(slot_scales[:, s0:s1], tok_scales[:].indirect(offs_sb[:, s0 // 16:s1 // 16]))
            if s1 < SLOTS:
                gather_words(last, s0, s1, T)
            else:
                gather_words(last, s0, s0 + C, T)
                gather_words(last, s0 + C, s1, T)

        for r in range(TOP):
            spread = psum.tile([P, T // P, P], F32, name="spread", tag="back", bufs=2)
            for c in range(T // P):
                nc.tensor.transpose(spread[:, c, :], gate_cols[:, r, c:c + 1].to_broadcast([P, P]), ident[:])
            nc.scalar.activation(gate_sb[r][:].rearrange("m (p c) -> m p c", p=P), spread[:].rearrange("m c p -> m p c"), COPY)

        def experts(b, pieces, tag, bufs, copy):
            first, end = PIECES[pieces[0]][0], PIECES[pieces[-1]][1]
            acc = psum.tile([P, (end - first) * C], F32, name="acc", tag=tag, bufs=bufs)
            for i in pieces:
                e0, e1, b0, b1 = PIECES[i]
                for e in range(e0, e1):
                    for a in range(PASSES):
                        col = (((e - e0) * PASSES + a) * (b1 - b0) + b - b0) * P * PACK
                        nc.tensor.matmul_mx(
                            out=acc[:, (e - first) * C:(e - first + 1) * C],
                            lhsT=w_sb[i][:, col:col + P * PACK].bitcast(FP8X4),
                            lhsT_scale=w_scale_sb[4 * a:, e * N + b * P:e * N + (b + 1) * P],
                            rhs=slot_words[a][:, e * C:(e + 1) * C].bitcast(FP8X4),
                            rhs_scale=slot_scales[4 * a:, e * C:(e + 1) * C],
                            start=(a == 0),
                            stop=(a == PASSES - 1),
                        )
            copy(y[b][:, first * C:end * C], acc[:])

        def gated(b, r, term, t0, t1):
            nc.vector.tensor_tensor(term[:, t0:t1], y[b][:].indirect(pos_sb[r][:, t0 // 16:t1 // 16]), gate_sb[r][:, t0:t1], MULT)

        for i in range(3):
            experts(0, [i], "acc", 3, scalar_copy)
        experts(0, [3], "after0", 1, nc.vector.tensor_copy)
        experts(1, [2, 3], "after0", 1, scalar_copy)
        experts(1, [4, 5], "acc", 3, scalar_copy)
        experts(1, [6], "acc", 3, scalar_copy)
        experts(1, [7], "late0", 1, scalar_copy)
        experts(2, [4], "late0", 1, scalar_copy)
        for i in range(8, 10):
            experts(2, [i], "acc", 3, scalar_copy)
        experts(2, [10], "after0", 1, scalar_copy)
        experts(2, [11], "late1", 1, scalar_copy)

        terms = [[keep.tile([P, T], F32, name="term%d_%d" % (b, r)) for r in range(TOP)] for b in range(BLOCKS)]
        for b in range(BLOCKS - 1):
            gated(b, 0, terms[b][0], 0, T)
            gated(b, 1, terms[b][1], 0, T)
            gated(b, 2, terms[b][2], 0, HALF)
            gated(b, 2, terms[b][2], HALF, T)

        for b in range(BLOCKS - 1):
            turned = psum.tile([P, T // P, P], F32, name="turned", tag="late%d" % b, bufs=1)
            for c in range(T // P):
                for r in range(TOP):
                    nc.tensor.matmul(turned[:, c, :], lhsT=terms[b][r][:, c * P:(c + 1) * P], rhs=ident[:],
                                     is_transpose=True, start=(r == 0), stop=(r == TOP - 1))
            turned_sb = keep.tile([P, T // P, P], F32, name="turned_sb%d" % b)
            nc.scalar.activation(turned_sb[:], turned[:], COPY)
            back = psum.tile([P, T], F32, name="back", tag=("after0", "back")[b], bufs=(1, 2)[b])
            for c in range(T // P):
                nc.tensor.transpose(back[:, c * P:(c + 1) * P], turned_sb[:, c, :], ident[:])
            total = keep.tile([P, T], F32, name="total%d" % b)
            nc.scalar.activation(total[:], back[:], COPY)
            nc.scalar.dma_start(out=out[b * P:(b + 1) * P, :], in_=total[:])

        b = BLOCKS - 1
        part = keep.tile([P, T], F32, name="part")
        total = keep.tile([P, T], F32, name="total_last")
        gated(b, 0, terms[b][0], 0, T)
        gated(b, 1, terms[b][1], 0, T)
        gated(b, 2, terms[b][2], 0, HALF)
        nc.vector.tensor_tensor(part[:], terms[b][0][:], terms[b][1][:], ADD)
        gated(b, 2, terms[b][2], HALF, T)
        for h in range(2):
            cols = slice(h * HALF, (h + 1) * HALF)
            nc.vector.tensor_tensor(total[:, cols], part[:, cols], terms[b][2][:, cols], ADD)
            nc.sync.dma_start(out=out[b * P:(b + 1) * P, cols], in_=total[:, cols])
